import numpy as np
import ml_dtypes


def mxq(x, axis, fmt="e4m3"):
    dtype, down = {"e4m3": (ml_dtypes.float8_e4m3fn, 7), "e5m2": (ml_dtypes.float8_e5m2, 14)}[fmt]
    v = np.moveaxis(np.asarray(x, np.float32).astype(ml_dtypes.bfloat16).astype(np.float64), axis, -1)
    blocks = v.reshape(v.shape[:-1] + (-1, 32))
    amax = np.abs(blocks).max(-1, keepdims=True)
    byte = np.maximum(np.where(amax > 0, np.frexp(amax)[1] - 1 + 127, 0) - down, 1)
    scale = np.exp2(byte - 127.0)
    codes = (blocks / scale).astype(np.float32).astype(dtype).astype(np.float64)
    return np.moveaxis((codes * scale).reshape(v.shape), -1, axis)


WIDE = False


def mx_kscale(k):
    if not WIDE:
        return np.ones(k)
    levels = np.array([10, -10, 5, -5, 0])
    if k % 512:
        return np.exp2(np.random.permutation(np.resize(levels, k // 32))).repeat(32)
    a = np.empty((k // 512, 16))
    for p in range(k // 512):
        a[p, :8] = np.random.permutation(np.resize(levels, 8))
        for g in range(8):
            far = levels[np.abs(levels - a[p, g]) >= 10]
            a[p, g + 8] = far[np.random.randint(len(far))]
    return np.exp2(a.ravel()).repeat(32)


BF16 = ml_dtypes.bfloat16


def bf(x):
    return np.asarray(x, np.float32).astype(BF16)


def f64(x):
    return np.asarray(x).astype(np.float64)


E2M1 = np.array([0.0, 0.5, 1.0, 1.5, 2.0, 3.0, 4.0, 6.0, -0.0, -0.5, -1.0, -1.5, -2.0, -3.0, -4.0, -6.0])


def pack_weight(w, fmt):
    k, n = w.shape
    w = f64(bf(w)).reshape(k // 32, 32, n)
    amax = np.abs(w).max(1)
    if fmt == "e4m3":
        byte = np.frexp(amax)[1] - 1 + 127 - 7
    else:
        mant, ex = np.frexp(amax / 6.0)
        byte = np.where(mant > 0.5, ex, ex - 1) + 127
    byte = np.clip(np.where(amax > 0, byte, 1), 1, 254)
    scaled = (w * np.exp2(127.0 - byte)[:, None, :]).reshape(k, n).astype(np.float32)
    by_word = np.ascontiguousarray(scaled.reshape(k // 512, 128, 4, n).transpose(0, 1, 3, 2))
    if fmt == "e4m3":
        words = by_word.astype(ml_dtypes.float8_e4m3fn).view(np.uint8)
    else:
        c = by_word.astype(ml_dtypes.float4_e2m1fn).view(np.uint8) & 0xF
        words = c[..., 0::2] | (c[..., 1::2] << 4)
    return np.ascontiguousarray(words), np.ascontiguousarray(byte.astype(np.uint8).reshape(k // 512, 16, n))


def unpack_weight(words, scales, fmt):
    g, p, n, _ = words.shape
    if fmt == "e4m3":
        vals = np.ascontiguousarray(words).view(ml_dtypes.float8_e4m3fn).astype(np.float64)
    else:
        nib = np.empty((g, p, n, 4), np.uint8)
        nib[..., 0::2] = words & 0xF
        nib[..., 1::2] = words >> 4
        vals = E2M1[nib]
    vals = vals * np.repeat(np.exp2(scales.astype(np.float64) - 127.0), 8, axis=1)[..., None]
    return vals.transpose(0, 1, 3, 2).reshape(g * 512, n)
def pack4(w):
    words, scales = pack_weight(w, "e2m1")
    return words.reshape(words.shape[0], 128, -1), scales


def unpack4(words, scales):
    return unpack_weight(words.reshape(words.shape[0], 128, -1, 2), scales, "e2m1")


def planes(Y):
    n, m = Y.shape
    b = f64(bf(Y)).reshape(n // 32, 32, m)
    amax = np.abs(b).max(1)
    byte = np.clip(np.where(amax > 0, np.frexp(amax)[1] - 1 + 127 - 7, 1), 1, 254)
    codes = (b * np.exp2(127.0 - byte)[:, None, :]).reshape(n, m).astype(np.float32).astype(ml_dtypes.float8_e4m3fn).view(np.uint8)
    words = codes.reshape(n // 512, 128, 4, m).transpose(0, 1, 3, 2)
    return np.ascontiguousarray(words), np.ascontiguousarray(byte.astype(np.uint8).reshape(n // 512, 16, m))


L, D, R = 4, 1024, 512

def symmetric(a):
    return (a + a.swapaxes(1, 2)) / np.sqrt(2.0)

def setup_inputs():
    rnd = np.random.standard_normal
    s = mx_kscale(L * D).reshape(L, D)
    c = np.exp(0.6 * rnd((L, R)))
    S = rnd((L, D, R)) / np.sqrt(D) * c[:, None, :]
    H = symmetric(rnd((L, D, D)))
    d = 3.0 * np.exp(0.3 * rnd((L, D)))
    M = c[:, :, None] * c[:, None, :] * symmetric(rnd((L, R, R)))
    mu = 0.6 * np.exp(0.2 * rnd((L,)))
    W = (H / s[:, :, None] / s[:, None, :]).reshape(L * D, D)
    h_words, h_scales = pack4(W)
    return {"dirs": bf(S * s[:, :, None]), "h_words": h_words, "h_scales": h_scales,
            "ridge": bf(d / s / s), "prev": bf(M), "carry": bf(mu)}

def reference(dirs, h_words, h_scales, ridge, prev, carry):
    S = f64(dirs)
    H = unpack4(h_words, h_scales).reshape(L, D, D)
    Sq = mxq(S, 1)
    U = (Sq.swapaxes(1, 2) @ H) + S.swapaxes(1, 2) * f64(ridge)[:, None, :]
    A = mxq(U, 2) @ Sq
    y = A + f64(carry)[:, None, None] * f64(prev)
    Y = y.reshape(L * R, R).T
    words, scales = planes(Y)
    return y, words, scales

@@ -1,0 +1,355 @@
+from contextlib import ExitStack
+
+import concourse.mybir as mybir
+from concourse.masks import make_identity
+
+L, D, R = 4, 1024, 512
+FLOPS = L * (2 * R * D * D + 2 * R * D * R)
+
+F32 = mybir.dt.float32
+BF16 = mybir.dt.bfloat16
+I32 = mybir.dt.int32
+U32 = mybir.dt.uint32
+U8 = mybir.dt.uint8
+FP8X4 = mybir.dt.float8_e4m3fn_x4
+FP4X4 = mybir.dt.float4_e2m1fn_x4
+MULT = mybir.AluOpType.mult
+ADD = mybir.AluOpType.add
+
+P = 128
+PACK = 4
+G = D // (P * PACK)
+RT = R // P
+NSIL = 2
+NHC = 4
+NCW = [3, 3, 2, 1, 1, 1]
+
+
+def tile_layerwise_subspace_newton_matrix_k7_kernel(
+    tc, dirs, h_words, h_scales, ridge, prev, carry, out_0, out_1, out_2
+):
+    nc = tc.nc
+    with ExitStack() as ctx:
+        sb = ctx.enter_context(tc.tile_pool(name="sb", bufs=1))
+        ps = ctx.enter_context(tc.psum_pool(name="ps", bufs=1))
+
+        def tiles(name, count, shape, dtype):
+            return [sb.tile(shape, dtype, name="%s%d" % (name, i), align_bytes=64) for i in range(count)]
+
+        s_raw = tiles("s_raw", L * G, [P, PACK, R], BF16)
+        s_il = tiles("s_il", NSIL, [P, R, PACK], BF16)
+        s_codes = tiles("s_codes", L * G, [P, R], U32)
+        s_scales = tiles("s_scales", L * G, [P, R], U8)
+        h_raw = tiles("h_raw", L * G, [P, 2 * D], U8)
+        h_cols = tiles("h_cols", NHC * G, [P, G, PACK, 2 * P], U8)
+        hs_raw = tiles("hs_raw", 1, [P, D], U8)[0]
+        hs_cols = tiles("hs_cols", L * G, [P, D], U8)
+        m_raw = tiles("m_raw", L, [P, RT, R], BF16)
+        d_col = tiles("d_col", 1, [P, L * G, PACK], BF16)[0]
+        mu = tiles("mu", 1, [P, L], BF16)[0]
+        ident = tiles("ident", 1, [P, P], F32)[0]
+        u_rows = tiles("u_rows", 2 * G, [P, 2, PACK, R // 2], BF16)
+        u_il = tiles("u_il", 2 * G, [P, R, PACK], BF16)
+        u_codes = tiles("u_codes", 2 * G, [P, R], U32)
+        u_scales = tiles("u_scales", 2 * G, [P, R], U8)
+        y = tiles("y", 2 * RT, [P, R], F32)
+        y_il = tiles("y_il", 2, [P, R, PACK], BF16)
+        y_codes = tiles("y_codes", L, [P, R], U32)
+        y_scales = tiles("y_scales", 1, [P, L * R], U8)[0]
+        u_bank = [ps.tile([P, R], F32, name="u_bank%d" % i) for i in range(PACK)]
+        a_bank = [ps.tile([P, R], F32, name="a_bank%d" % i) for i in range(2)]
+        t_bank = [ps.tile([P, R], F32, name="t_bank%d" % i) for i in range(2)]
+
+        def abank(b, a):
+            return u_bank[a] if b == L - 1 else a_bank[a % 2]
+
+        def tbank(b, a):
+            return a_bank[a % 2] if b == L - 1 and a >= 2 else t_bank[a % 2]
+
+        def load_s(b, g):
+            rows = dirs[b, 512 * g : 512 * (g + 1), :]
+            nc.sync.dma_start(out=s_raw[G * b + g][:], in_=rows.rearrange("(p t) r -> p t r", t=PACK))
+
+        def load_h(b, g):
+            nc.sync.dma_start(out=h_raw[G * b + g][:].bitcast(I32), in_=h_words[G * b + g].bitcast(I32))
+
+        def load_hs():
+            for q in range(4):
+                nc.sync.dma_start(
+                    out=hs_raw[32 * q : 32 * (q + 1), :].bitcast(I32),
+                    in_=h_scales[:, 4 * q : 4 * q + 4, :].bitcast(I32),
+                )
+
+        def shift_hs(k, eng):
+            eng.dma_start(out=hs_cols[k][0:100, :].bitcast(I32), in_=hs_cols[0][4 * k : 4 * k + 100, :].bitcast(I32))
+
+        def load_m(b):
+            nc.sync.dma_start(out=m_raw[b][:], in_=prev[b].rearrange("(a p) s -> p a s", p=P))
+
+        def interleave(eng, dst, src, c0, c1):
+            out = dst[:, c0:c1, :].rearrange("p (c i) t -> p c t i", i=4)
+            in_ = src[:, :, c0:c1].rearrange("p t (c i) -> p c t i", i=4)
+            if eng == "V":
+                nc.vector.tensor_copy(out=out, in_=in_)
+            elif eng == "S":
+                nc.scalar.copy(out=out, in_=in_)
+            else:
+                nc.gpsimd.tensor_scalar(out=out, in0=in_, scalar1=1.0, scalar2=0.0, op0=MULT, op1=ADD)
+
+        def A(eng, b, g, c0=0, c1=R):
+            interleave(eng, s_il[(G * b + g) % NSIL], s_raw[G * b + g], c0, c1)
+
+        def B(b, g):
+            k = G * b + g
+            nc.vector.quantize_mx(
+                out=s_codes[k][:].bitcast(FP8X4),
+                scales=s_scales[k][:],
+                in_=s_il[k % NSIL][:].rearrange("p r t -> p (r t)"),
+            )
+
+        def CW(b, h, g, eng="V"):
+            src = h_raw[G * b + g][:, D * h : D * (h + 1)].rearrange("p (m t e) -> p t m e", t=PACK, e=2)
+            dst = h_cols[G * (b % NHC) + h][:, g, :, :].rearrange("p t (m e) -> p t m e", e=2)
+            (nc.vector if eng == "V" else nc.gpsimd).tensor_copy(out=dst, in_=src)
+
+        def CS():
+            src = hs_raw[:].rearrange("p (h m t) -> p h t m", h=G, t=PACK)
+            dst = hs_cols[0][:].rearrange("p (h t m) -> p h t m", h=G, t=PACK)
+            nc.vector.tensor_copy(out=dst, in_=src)
+
+        def M1(b, h, t, gs=(0, 1)):
+            for g in gs:
+                nc.tensor.matmul_mx(
+                    out=u_bank[t][:],
+                    lhsT=h_cols[G * (b % NHC) + h][:, g, t, :].bitcast(FP4X4),
+                    lhsT_scale=hs_cols[G * b + g][:, P * (PACK * h + t) : P * (PACK * h + t + 1)],
+                    rhs=s_codes[G * b + g][:].bitcast(FP8X4),
+                    rhs_scale=s_scales[G * b + g][:],
+                    start=(g == 0),
+                    stop=(g == G - 1),
+                )
+
+        def Dd(b, h, t, f0=0, f1=2):
+            cols = slice(256 * f0, 256 * f1)
+            nc.vector.scalar_tensor_tensor(
+                out=u_rows[G * (b % 2) + h][:, f0:f1, t, :],
+                in0=s_raw[G * b + h][:, t, cols].rearrange("p (f r) -> p f r", r=256),
+                scalar=d_col[:, G * b + h, t : t + 1],
+                in1=u_bank[t][:, cols].rearrange("p (f r) -> p f r", r=256),
+                op0=MULT,
+                op1=ADD,
+            )
+
+        def J(eng, b, h, f, c0=0, c1=256):
+            k = G * (b % 2) + h
+            interleave(eng, u_il[k][:, 256 * f : 256 * (f + 1), :], u_rows[k][:, f, :, :], c0, c1)
+
+        def E(b, h, c0=0, c1=R):
+            k = G * (b % 2) + h
+            nc.vector.quantize_mx(
+                out=u_codes[k][:, c0:c1].bitcast(FP8X4),
+                scales=u_scales[k][:, c0:c1],
+                in_=u_il[k][:, c0:c1, :].rearrange("p r t -> p (r t)"),
+            )
+
+        def M2(b, a):
+            cols = slice(P * a, P * (a + 1))
+            for h in range(G):
+                k = G * (b % 2) + h
+                nc.tensor.matmul_mx(
+                    out=abank(b, a)[:],
+                    lhsT=u_codes[k][:, cols].bitcast(FP8X4),
+                    lhsT_scale=u_scales[k][:, cols],
+                    rhs=s_codes[G * b + h][:].bitcast(FP8X4),
+                    rhs_scale=s_scales[G * b + h][:],
+                    start=(h == 0),
+                    stop=(h == G - 1),
+                )
+
+        def F(b, a):
+            nc.vector.scalar_tensor_tensor(
+                out=y[RT * (b % 2) + a][:],
+                in0=m_raw[b][:, a, :],
+                scalar=mu[:, b : b + 1],
+                in1=abank(b, a)[:],
+                op0=MULT,
+                op1=ADD,
+            )
+
+        def store_y(b, a):
+            nc.sync.dma_start(out=out_0[b, P * a : P * (a + 1), :], in_=y[RT * (b % 2) + a][:])
+
+        def T(b, a):
+            for t in range(PACK):
+                nc.tensor.transpose(
+                    tbank(b, a)[:, P * t : P * (t + 1)], y[RT * (b % 2) + a][:, t:R:PACK], ident[:]
+                )
+
+        def H(b, a, eng="S"):
+            (nc.scalar.copy if eng == "S" else nc.vector.tensor_copy)(
+                out=y_il[b % 2][:, P * a : P * (a + 1), :],
+                in_=tbank(b, a)[:].rearrange("p (t r) -> p r t", t=PACK),
+            )
+
+        def I(b, c0=0, c1=R):
+            nc.vector.quantize_mx(
+                out=y_codes[b][:, c0:c1].bitcast(FP8X4),
+                scales=y_scales[:, R * b + c0 : R * b + c1],
+                in_=y_il[b % 2][:, c0:c1, :].rearrange("p r t -> p (r t)"),
+            )
+
+        def store_codes(b, c0=0, c1=R):
+            dst = out_1[0, :, R * b + c0 : R * b + c1, :].rearrange("p m t -> p (m t)").bitcast(I32)
+            nc.sync.dma_start(out=dst, in_=y_codes[b][:, c0:c1].bitcast(I32))
+
+        def store_scales(c0, c1, eng):
+            for q in range(4):
+                eng.dma_start(
+                    out=out_2[0, 4 * q : 4 * q + 4, c0:c1].bitcast(I32),
+                    in_=y_scales[32 * q : 32 * q + 4, c0:c1].bitcast(I32),
+                )
+
+        ctx.enter_context(tc.manual_schedule())
+
+        nc.scalar.dma_start(out=d_col[:], in_=ridge.rearrange("b (g p t) -> p (b g) t", p=P, t=PACK))
+        nc.scalar.dma_start(out=mu[:], in_=carry.partition_broadcast(P))
+        for k in range(1, L * G):
+            nc.vector.memset(hs_cols[k][:].bitcast(I32), 0)
+        make_identity(nc, ident[:])
+        load_hs()
+        load_h(0, 0)
+        load_s(0, 0)
+        CS()
+        shift_hs(1, nc.scalar)
+        load_h(0, 1)
+        load_s(0, 1)
+        load_s(1, 0)
+        load_h(1, 0)
+        load_h(1, 1)
+        for k in range(2, 4):
+            shift_hs(k, nc.sync)
+        load_s(1, 1)
+        load_m(0)
+        for k in range(4, L * G):
+            shift_hs(k, nc.sync)
+        for b in range(2, L):
+            for g in range(G):
+                load_h(b, g)
+            for g in range(G):
+                load_s(b, g)
+            load_m(b - 1)
+        load_m(L - 1)
+
+        CW(0, 0, 0)
+        CW(0, 1, 0)
+        A("S", 0, 0, 0, 256)
+        A("V", 0, 0, 256, 512)
+        CW(0, 0, 1)
+        B(0, 0)
+        for t in range(PACK):
+            M1(0, 0, t, (0,))
+        A("S", 0, 1, 0, 320)
+        A("V", 0, 1, 320, 512)
+        CW(0, 1, 1)
+        B(0, 1)
+        for t in range(PACK):
+            M1(0, 0, t, (1,))
+        cw = [(b, h, g) for b in range(1, L) for h in range(G) for g in range(G)]
+
+        for s in range(L * G - 2):
+            b, h = divmod(s, G)
+            a0 = 2 * h
+            if s == 0:
+                CW(*cw.pop(0))
+            A("S", b + 1, h)
+            for t in range(PACK):
+                Dd(b, h, t)
+                if t == 0 and s > 0:
+                    E(*divmod(s - 1, G))
+                    if b > 0:
+                        M2(b - 1, a0)
+                        M2(b - 1, a0 + 1)
+                if h == 0 and t < 3:
+                    M1(b, 1, t)
+                if h == 1:
+                    M1(b + 1, 0, t, (0,))
+            J("S", b, h, 0)
+            J("S", b, h, 1)
+            if b > 0:
+                for a in (a0, a0 + 1):
+                    F(b - 1, a)
+                    store_y(b - 1, a)
+                    T(b - 1, a)
+                    H(b - 1, a)
+            if h == 0:
+                M1(b, 1, 3)
+            if h == 1:
+                B(b + 1, h)
+                for t in range(PACK):
+                    M1(b + 1, 0, t, (1,))
+            for i in range(NCW[s]):
+                CW(*cw.pop(0))
+            if h == 0:
+                B(b + 1, h)
+            if s >= 3:
+                c = 256 * (1 - h)
+                I((s - 3) // 2, c, c + 256)
+                store_codes((s - 3) // 2, c, c + 256)
+
+        b = L - 1
+        for t in range(PACK):
+            Dd(b, 0, t)
+            if t == 0:
+                E(b - 1, 1)
+                M2(b - 1, 0)
+                M2(b - 1, 1)
+            M1(b, 1, t)
+        J("S", b, 0, 0)
+        J("S", b, 0, 1)
+        for a in (0, 1):
+            F(b - 1, a)
+            store_y(b - 1, a)
+            M2(b - 1, a + 2)
+        T(b - 1, 0)
+        T(b - 1, 1)
+        for t in range(PACK):
+            Dd(b, 1, t, 0, 1)
+        H(b - 1, 0)
+        H(b - 1, 1)
+        J("S", b, 1, 0, 0, 128)
+        J("S", b, 1, 0, 128, 256)
+        for a in (2, 3):
+            F(b - 1, a)
+            store_y(b - 1, a)
+            T(b - 1, a)
+        E(b, 0)
+        for t in range(PACK):
+            Dd(b, 1, t, 1, 2)
+        E(b, 1, 0, 256)
+        M2(b, 0)
+        M2(b, 1)
+        J("S", b, 1, 1, 0, 128)
+        J("V", b, 1, 1, 128, 256)
+        H(b - 1, 2)
+        H(b - 1, 3)
+        I(b - 2, 256, 512)
+        store_codes(b - 2, 256, 512)
+        E(b, 1, 256, 512)
+        M2(b, 2)
+        M2(b, 3)
+        for a in range(RT):
+            F(b, a)
+            store_y(b, a)
+            T(b, a)
+        I(b - 1)
+        store_codes(b - 1)
+        store_scales(0, R * b, nc.sync)
+        H(b, 0)
+        H(b, 1)
+        H(b, 2)
+        I(b, 0, 256)
+        H(b, 3, "V")
+        store_codes(b, 0, 256)
+        I(b, 256, 512)
+        store_codes(b, 256, 512)
+        store_scales(R * b, R * L, nc.scalar)

@@ -22,7 +22,10 @@ G = D // (P * PACK)
 RT = R // P
 NSIL = 2
 NHC = 4
-NCW = [3, 3, 2, 1, 1, 1]
+AG = [128, 128, 16, 32, 32, 32]
+AS = [512, 256, 512, 384, 384, 384]
+NG = [1, 1, 1, 2, 2, 2]
+NCW = [0, 0, 1, 0, 0, 0]
 
 
 def tile_layerwise_subspace_newton_matrix_k7_kernel(
@@ -53,6 +56,7 @@ def tile_layerwise_subspace_newton_matrix_k7_kernel(
         u_codes = tiles("u_codes", 2 * G, [P, R], U32)
         u_scales = tiles("u_scales", 2 * G, [P, R], U8)
         y = tiles("y", 2 * RT, [P, R], F32)
+        y_bf = tiles("y_bf", RT, [P, R], BF16)
         y_il = tiles("y_il", 2, [P, R, PACK], BF16)
         y_codes = tiles("y_codes", L, [P, R], U32)
         y_scales = tiles("y_scales", 1, [P, L * R], U8)[0]
@@ -64,7 +68,7 @@ def tile_layerwise_subspace_newton_matrix_k7_kernel(
             return u_bank[a] if b == L - 1 else a_bank[a % 2]
 
         def tbank(b, a):
-            return a_bank[a % 2] if b == L - 1 and a >= 2 else t_bank[a % 2]
+            return [t_bank[0], a_bank[0], t_bank[1], a_bank[1]][a] if b == L - 1 else t_bank[a // 2]
 
         def load_s(b, g):
             rows = dirs[b, 512 * g : 512 * (g + 1), :]
@@ -97,14 +101,14 @@ def tile_layerwise_subspace_newton_matrix_k7_kernel(
                 nc.gpsimd.tensor_scalar(out=out, in0=in_, scalar1=1.0, scalar2=0.0, op0=MULT, op1=ADD)
 
         def A(eng, b, g, c0=0, c1=R):
-            interleave(eng, s_il[(G * b + g) % NSIL], s_raw[G * b + g], c0, c1)
+            interleave(eng, s_il[min(G * b + g, 1)], s_raw[G * b + g], c0, c1)
 
         def B(b, g):
             k = G * b + g
             nc.vector.quantize_mx(
                 out=s_codes[k][:].bitcast(FP8X4),
                 scales=s_scales[k][:],
-                in_=s_il[k % NSIL][:].rearrange("p r t -> p (r t)"),
+                in_=s_il[min(k, 1)][:].rearrange("p r t -> p (r t)"),
             )
 
         def CW(b, h, g, eng="V"):
@@ -179,16 +183,30 @@ def tile_layerwise_subspace_newton_matrix_k7_kernel(
         def store_y(b, a):
             nc.sync.dma_start(out=out_0[b, P * a : P * (a + 1), :], in_=y[RT * (b % 2) + a][:])
 
+        def K(b, a, eng="S"):
+            out = y_bf[a][:].rearrange("r (u p e) -> r u p e", u=2, e=2)
+            in_ = y[RT * (b % 2) + a][:].rearrange("r (p u e) -> r u p e", u=2, e=2)
+            if eng == "V":
+                nc.vector.tensor_copy(out=out, in_=in_)
+            elif eng == "S":
+                nc.scalar.copy(out=out, in_=in_)
+            else:
+                nc.gpsimd.tensor_scalar(out=out, in0=in_, scalar1=1.0, scalar2=0.0, op0=MULT, op1=ADD)
+
         def T(b, a):
-            for t in range(PACK):
+            for u in range(2):
+                c = P * (2 * (a % 2) + u)
                 nc.tensor.transpose(
-                    tbank(b, a)[:, P * t : P * (t + 1)], y[RT * (b % 2) + a][:, t:R:PACK], ident[:]
+                    tbank(b, a)[:, c : c + P], y_bf[a][:].bitcast(F32)[:, P * u : P * (u + 1)], ident[:]
                 )
 
-        def H(b, a, eng="S"):
-            (nc.scalar.copy if eng == "S" else nc.vector.tensor_copy)(
-                out=y_il[b % 2][:, P * a : P * (a + 1), :],
-                in_=tbank(b, a)[:].rearrange("p (t r) -> p r t", t=PACK),
+        def H(b, a0, a1, eng="S"):
+            copy = nc.scalar.copy if eng == "S" else nc.vector.tensor_copy
+            words = y_il[b % 2][:, P * a0 : P * a1, :].rearrange("p r t -> p (r t)").bitcast(F32)
+            src = tbank(b, a0)[:, 2 * P * (a0 % 2) : 2 * P * (a0 % 2 + a1 - a0)]
+            copy(
+                out=words.rearrange("p (a r u) -> p a r u", r=P, u=2),
+                in_=src.rearrange("p (a u r) -> p a r u", r=P, u=2),
             )
 
         def I(b, c0=0, c1=R):
@@ -256,100 +274,155 @@ def tile_layerwise_subspace_newton_matrix_k7_kernel(
             M1(0, 0, t, (1,))
         cw = [(b, h, g) for b in range(1, L) for h in range(G) for g in range(G)]
 
-        for s in range(L * G - 2):
+        def finish(b, a):
+            F(b, a)
+            store_y(b, a)
+
+        def prefetch(s):
             b, h = divmod(s, G)
-            a0 = 2 * h
-            if s == 0:
+            A("G", b + 1, h, 0, AG[s])
+            for i in range(NG[s]):
+                CW(*cw.pop(0), "G")
+
+        def fills(s):
+            b, h = divmod(s, G)
+            if AS[s] < R:
+                A("V", b + 1, h, AS[s], R)
+            if s == 1:
                 CW(*cw.pop(0))
-            A("S", b + 1, h)
-            for t in range(PACK):
-                Dd(b, h, t)
-                if t == 0 and s > 0:
-                    E(*divmod(s - 1, G))
-                    if b > 0:
-                        M2(b - 1, a0)
-                        M2(b - 1, a0 + 1)
-                if h == 0 and t < 3:
-                    M1(b, 1, t)
-                if h == 1:
-                    M1(b + 1, 0, t, (0,))
-            J("S", b, h, 0)
-            J("S", b, h, 1)
-            if b > 0:
-                for a in (a0, a0 + 1):
-                    F(b - 1, a)
-                    store_y(b - 1, a)
-                    T(b - 1, a)
-                    H(b - 1, a)
-            if h == 0:
-                M1(b, 1, 3)
-            if h == 1:
                 B(b + 1, h)
                 for t in range(PACK):
                     M1(b + 1, 0, t, (1,))
+            if s > 0:
+                E(*divmod(s - 1, G))
+            if h == 0 and b > 0:
+                M2(b - 1, 0)
+                M2(b - 1, 1)
+            if b > 1:
+                I(b - 2, 256 * h, 256 * h + 256)
+                store_codes(b - 2, 256 * h, 256 * h + 256)
             for i in range(NCW[s]):
                 CW(*cw.pop(0))
-            if h == 0:
+            if s != 1:
                 B(b + 1, h)
-            if s >= 3:
-                c = 256 * (1 - h)
-                I((s - 3) // 2, c, c + 256)
-                store_codes((s - 3) // 2, c, c + 256)
+
+        CW(*cw.pop(0))
+        for b in range(L - 1):
+            s = 2 * b
+            prefetch(s)
+            if b > 1:
+                K(b - 2, 0)
+                K(b - 2, 1)
+                T(b - 2, 0)
+                T(b - 2, 1)
+            A("S", b + 1, 0, AG[s], AS[s])
+            if b > 1:
+                finish(b - 2, 2)
+                finish(b - 2, 3)
+                H(b - 2, 0, 2)
+                K(b - 2, 2)
+                K(b - 2, 3)
+            for t in range(PACK):
+                Dd(b, 0, t)
+                M1(b, 1, t)
+            J("S", b, 0, 0)
+            J("S", b, 0, 1)
+            fills(s)
+            s += 1
+            prefetch(s)
+            if b > 1:
+                T(b - 2, 2)
+                T(b - 2, 3)
+                H(b - 2, 2, 4)
+            A("S", b + 1, 1, AG[s], AS[s])
+            for t in range(PACK):
+                Dd(b, 1, t)
+                M1(b + 1, 0, t, (0,))
+            J("S", b, 1, 0)
+            J("S", b, 1, 1)
+            if b > 0:
+                for a in (0, 1):
+                    finish(b - 1, a)
+                    M2(b - 1, a + 2)
+            fills(s)
+            if s != 1:
+                for t in range(PACK):
+                    M1(b + 1, 0, t, (1,))
+        assert not cw
 
         b = L - 1
+        K(b - 2, 0)
+        K(b - 2, 1)
+        finish(b - 2, 2)
+        finish(b - 2, 3)
+        K(b - 2, 2, "G")
+        K(b - 2, 3, "G")
         for t in range(PACK):
-            Dd(b, 0, t)
-            if t == 0:
+            if t == 3:
                 E(b - 1, 1)
                 M2(b - 1, 0)
                 M2(b - 1, 1)
+            Dd(b, 0, t)
             M1(b, 1, t)
+            if t == 1:
+                T(b - 2, 0)
+                T(b - 2, 1)
+                H(b - 2, 0, 2)
         J("S", b, 0, 0)
         J("S", b, 0, 1)
+        T(b - 2, 2)
+        T(b - 2, 3)
+        Dd(b, 1, 0, 0, 1)
+        Dd(b, 1, 1, 0, 1)
         for a in (0, 1):
-            F(b - 1, a)
-            store_y(b - 1, a)
+            finish(b - 1, a)
+            K(b - 1, a, "G")
             M2(b - 1, a + 2)
-        T(b - 1, 0)
-        T(b - 1, 1)
-        for t in range(PACK):
-            Dd(b, 1, t, 0, 1)
-        H(b - 1, 0)
-        H(b - 1, 1)
+        Dd(b, 1, 2, 0, 1)
+        Dd(b, 1, 3, 0, 1)
         J("S", b, 1, 0, 0, 128)
         J("S", b, 1, 0, 128, 256)
-        for a in (2, 3):
-            F(b - 1, a)
-            store_y(b - 1, a)
-            T(b - 1, a)
-        E(b, 0)
         for t in range(PACK):
             Dd(b, 1, t, 1, 2)
+        J("S", b, 1, 1, 0, 128)
+        H(b - 2, 2, 4)
+        T(b - 1, 0)
+        T(b - 1, 1)
+        finish(b - 1, 2)
+        K(b - 1, 2)
+        E(b, 0)
         E(b, 1, 0, 256)
         M2(b, 0)
         M2(b, 1)
-        J("S", b, 1, 1, 0, 128)
         J("V", b, 1, 1, 128, 256)
-        H(b - 1, 2)
-        H(b - 1, 3)
-        I(b - 2, 256, 512)
-        store_codes(b - 2, 256, 512)
+        finish(b - 1, 3)
         E(b, 1, 256, 512)
         M2(b, 2)
         M2(b, 3)
-        for a in range(RT):
-            F(b, a)
-            store_y(b, a)
-            T(b, a)
+        K(b - 1, 3)
+        H(b - 1, 0, 2)
+        T(b - 1, 2)
+        T(b - 1, 3)
+        I(b - 2)
+        store_codes(b - 2)
+        store_scales(0, R * (b - 1), nc.sync)
+        finish(b, 0)
+        K(b, 0)
+        H(b - 1, 2, 4)
+        for a in range(1, RT):
+            finish(b, a)
+            if a < 3:
+                K(b, a)
         I(b - 1)
         store_codes(b - 1)
-        store_scales(0, R * b, nc.sync)
-        H(b, 0)
-        H(b, 1)
-        H(b, 2)
-        I(b, 0, 256)
-        H(b, 3, "V")
-        store_codes(b, 0, 256)
+        K(b, 3, "V")
+        for a in range(RT):
+            T(b, a)
+        for a in range(RT):
+            H(b, a, a + 1, "V" if a == 3 else "S")
+            if a == 1:
+                I(b, 0, 256)
+                store_codes(b, 0, 256)
         I(b, 256, 512)
         store_codes(b, 256, 512)
-        store_scales(R * b, R * L, nc.scalar)
+        store_scales(R * (b - 1), R * L, nc.scalar)

@@ -22,10 +22,12 @@ G = D // (P * PACK)
 RT = R // P
 NSIL = 2
 NHC = 4
-AG = [128, 128, 16, 32, 32, 32]
-AS = [512, 256, 512, 384, 384, 384]
+AG = [128, 128, 32, 32, 32]
 NG = [1, 1, 1, 2, 2, 2]
-NCW = [0, 0, 1, 0, 0, 0]
+NCW = [1, 0, 1, 0, 0, 0]
+ALIAS = {(0, 2): 0}
+WN = 128
+DIRECT = set()
 
 
 def tile_layerwise_subspace_newton_matrix_k7_kernel(
@@ -48,6 +50,7 @@ def tile_layerwise_subspace_newton_matrix_k7_kernel(
         hs_raw = tiles("hs_raw", 1, [P, D], U8)[0]
         hs_cols = tiles("hs_cols", L * G, [P, D], U8)
         m_raw = tiles("m_raw", L, [P, RT, R], BF16)
+        d_rows = tiles("d_rows", 1, [P, 512], BF16)[0]
         d_col = tiles("d_col", 1, [P, L * G, PACK], BF16)[0]
         mu = tiles("mu", 1, [P, L], BF16)[0]
         ident = tiles("ident", 1, [P, P], F32)[0]
@@ -56,7 +59,7 @@ def tile_layerwise_subspace_newton_matrix_k7_kernel(
         u_codes = tiles("u_codes", 2 * G, [P, R], U32)
         u_scales = tiles("u_scales", 2 * G, [P, R], U8)
         y = tiles("y", 2 * RT, [P, R], F32)
-        y_bf = tiles("y_bf", RT, [P, R], BF16)
+        y_bf = tiles("y_bf", 2 * RT, [P, R], BF16)
         y_il = tiles("y_il", 2, [P, R, PACK], BF16)
         y_codes = tiles("y_codes", L, [P, R], U32)
         y_scales = tiles("y_scales", 1, [P, L * R], U8)[0]
@@ -68,7 +71,10 @@ def tile_layerwise_subspace_newton_matrix_k7_kernel(
             return u_bank[a] if b == L - 1 else a_bank[a % 2]
 
         def tbank(b, a):
-            return [t_bank[0], a_bank[0], t_bank[1], a_bank[1]][a] if b == L - 1 else t_bank[a // 2]
+            return [t_bank[0], a_bank[0], t_bank[1], a_bank[1]][a] if b == L - 1 else t_bank[a % 2 if DIRECT else a // 2]
+
+        def sbuf(k):
+            return k % 2 if k < 2 else (k + 1) % 2
 
         def load_s(b, g):
             rows = dirs[b, 512 * g : 512 * (g + 1), :]
@@ -87,6 +93,19 @@ def tile_layerwise_subspace_newton_matrix_k7_kernel(
         def shift_hs(k, eng):
             eng.dma_start(out=hs_cols[k][0:100, :].bitcast(I32), in_=hs_cols[0][4 * k : 4 * k + 100, :].bitcast(I32))
 
+        def load_d():
+            nc.sync.dma_start(out=d_rows[0 : L * G, :], in_=ridge.rearrange("b (g j) -> (b g) j", g=G))
+
+        def turn_d():
+            for u in range(2):
+                nc.tensor.transpose(a_bank[0][:, P * u : P * (u + 1)], d_rows[:].bitcast(F32)[:, u:256:2], ident[:])
+
+        def copy_d():
+            nc.scalar.copy(
+                out=d_col[:].rearrange("p k t -> p (k t)").bitcast(F32).rearrange("p (k u) -> p k u", u=2),
+                in_=a_bank[0][:, 0:256].rearrange("p (u k) -> p k u", u=2)[:, 0 : L * G, :],
+            )
+
         def load_m(b):
             nc.sync.dma_start(out=m_raw[b][:], in_=prev[b].rearrange("(a p) s -> p a s", p=P))
 
@@ -101,14 +120,14 @@ def tile_layerwise_subspace_newton_matrix_k7_kernel(
                 nc.gpsimd.tensor_scalar(out=out, in0=in_, scalar1=1.0, scalar2=0.0, op0=MULT, op1=ADD)
 
         def A(eng, b, g, c0=0, c1=R):
-            interleave(eng, s_il[min(G * b + g, 1)], s_raw[G * b + g], c0, c1)
+            interleave(eng, s_il[(G * b + g) % 2], s_raw[G * b + g], c0, c1)
 
         def B(b, g):
             k = G * b + g
             nc.vector.quantize_mx(
                 out=s_codes[k][:].bitcast(FP8X4),
                 scales=s_scales[k][:],
-                in_=s_il[min(k, 1)][:].rearrange("p r t -> p (r t)"),
+                in_=s_il[k % 2][:].rearrange("p r t -> p (r t)"),
             )
 
         def CW(b, h, g, eng="V"):
@@ -156,9 +175,9 @@ def tile_layerwise_subspace_newton_matrix_k7_kernel(
                 in_=u_il[k][:, c0:c1, :].rearrange("p r t -> p (r t)"),
             )
 
-        def M2(b, a):
+        def M2(b, a, hs=(0, 1)):
             cols = slice(P * a, P * (a + 1))
-            for h in range(G):
+            for h in hs:
                 k = G * (b % 2) + h
                 nc.tensor.matmul_mx(
                     out=abank(b, a)[:],
@@ -183,9 +202,16 @@ def tile_layerwise_subspace_newton_matrix_k7_kernel(
         def store_y(b, a):
             nc.sync.dma_start(out=out_0[b, P * a : P * (a + 1), :], in_=y[RT * (b % 2) + a][:])
 
-        def K(b, a, eng="S"):
-            out = y_bf[a][:].rearrange("r (u p e) -> r u p e", u=2, e=2)
-            in_ = y[RT * (b % 2) + a][:].rearrange("r (p u e) -> r u p e", u=2, e=2)
+        def ybf(b, a):
+            if (b, a) in ALIAS:
+                return s_il[ALIAS[(b, a)]][:, 0:P, :].rearrange("p r t -> p (r t)")
+            return y_bf[RT * (b % 2) + a][:]
+
+        def K(b, a, eng="S", u0=0, u1=2):
+            if (b, a) in DIRECT:
+                return
+            out = ybf(b, a).rearrange("r (u p e) -> r u p e", u=2, e=2)[:, u0:u1]
+            in_ = y[RT * (b % 2) + a][:].rearrange("r (p u e) -> r u p e", u=2, e=2)[:, u0:u1]
             if eng == "V":
                 nc.vector.tensor_copy(out=out, in_=in_)
             elif eng == "S":
@@ -193,14 +219,38 @@ def tile_layerwise_subspace_newton_matrix_k7_kernel(
             else:
                 nc.gpsimd.tensor_scalar(out=out, in0=in_, scalar1=1.0, scalar2=0.0, op0=MULT, op1=ADD)
 
+        def FK(b, a):
+            for u in range(2):
+                nc.vector.scalar_tensor_tensor(
+                    out=ybf(b, a)[:, 256 * u : 256 * (u + 1)].rearrange("r (p e) -> r p e", e=2),
+                    in0=m_raw[b][:, a, :].rearrange("r (p u e) -> r u p e", u=2, e=2)[:, u],
+                    scalar=mu[:, b : b + 1],
+                    in1=abank(b, a)[:].rearrange("r (p u e) -> r u p e", u=2, e=2)[:, u],
+                    op0=MULT,
+                    op1=ADD,
+                )
+
         def T(b, a):
+            if (b, a) in DIRECT:
+                for t in range(PACK):
+                    nc.tensor.transpose(tbank(b, a)[:, P * t : P * (t + 1)], y[RT * (b % 2) + a][:, t:R:PACK], ident[:])
+                return
             for u in range(2):
                 c = P * (2 * (a % 2) + u)
                 nc.tensor.transpose(
-                    tbank(b, a)[:, c : c + P], y_bf[a][:].bitcast(F32)[:, P * u : P * (u + 1)], ident[:]
+                    tbank(b, a)[:, c : c + P], ybf(b, a).bitcast(F32)[:, P * u : P * (u + 1)], ident[:]
                 )
 
         def H(b, a0, a1, eng="S"):
+            if DIRECT and a1 - a0 == 2:
+                H(b, a0, a0 + 1, eng)
+                H(b, a0 + 1, a1, eng)
+                return
+            if (b, a0) in DIRECT:
+                nc.scalar.copy(
+                    out=y_il[b % 2][:, P * a0 : P * a1, :], in_=tbank(b, a0)[:].rearrange("p (t r) -> p r t", t=PACK)
+                )
+                return
             copy = nc.scalar.copy if eng == "S" else nc.vector.tensor_copy
             words = y_il[b % 2][:, P * a0 : P * a1, :].rearrange("p r t -> p (r t)").bitcast(F32)
             src = tbank(b, a0)[:, 2 * P * (a0 % 2) : 2 * P * (a0 % 2 + a1 - a0)]
@@ -220,58 +270,65 @@ def tile_layerwise_subspace_newton_matrix_k7_kernel(
             dst = out_1[0, :, R * b + c0 : R * b + c1, :].rearrange("p m t -> p (m t)").bitcast(I32)
             nc.sync.dma_start(out=dst, in_=y_codes[b][:, c0:c1].bitcast(I32))
 
-        def store_scales(c0, c1, eng):
+        def store_scales(c0, c1, engs):
             for q in range(4):
-                eng.dma_start(
+                engs[q % len(engs)].dma_start(
                     out=out_2[0, 4 * q : 4 * q + 4, c0:c1].bitcast(I32),
                     in_=y_scales[32 * q : 32 * q + 4, c0:c1].bitcast(I32),
                 )
 
         ctx.enter_context(tc.manual_schedule())
 
-        nc.scalar.dma_start(out=d_col[:], in_=ridge.rearrange("b (g p t) -> p (b g) t", p=P, t=PACK))
-        nc.scalar.dma_start(out=mu[:], in_=carry.partition_broadcast(P))
+        make_identity(nc, ident[:])
+        nc.vector.memset(d_rows[:].bitcast(I32), 0)
         for k in range(1, L * G):
             nc.vector.memset(hs_cols[k][:].bitcast(I32), 0)
-        make_identity(nc, ident[:])
         load_hs()
+        load_d()
+        turn_d()
+        copy_d()
         load_h(0, 0)
         load_s(0, 0)
-        CS()
-        shift_hs(1, nc.scalar)
-        load_h(0, 1)
         load_s(0, 1)
+        load_h(0, 1)
+        CS()
+        shift_hs(1, nc.sync)
         load_s(1, 0)
         load_h(1, 0)
+        load_s(1, 1)
         load_h(1, 1)
         for k in range(2, 4):
             shift_hs(k, nc.sync)
-        load_s(1, 1)
+        load_s(2, 0)
         load_m(0)
+        nc.sync.dma_start(out=mu[:], in_=carry.partition_broadcast(P))
+        load_h(2, 0)
+        load_h(2, 1)
+        load_s(2, 1)
         for k in range(4, L * G):
             shift_hs(k, nc.sync)
-        for b in range(2, L):
-            for g in range(G):
-                load_h(b, g)
-            for g in range(G):
-                load_s(b, g)
-            load_m(b - 1)
-        load_m(L - 1)
+        load_s(3, 0)
+        load_h(3, 0)
+        load_h(3, 1)
+        load_s(3, 1)
+        for b in range(1, L):
+            load_m(b)
 
         CW(0, 0, 0)
         CW(0, 1, 0)
-        A("S", 0, 0, 0, 256)
-        A("V", 0, 0, 256, 512)
-        CW(0, 0, 1)
+        A("S", 0, 0, 0, 192)
+        A("V", 0, 0, 192, 512)
         B(0, 0)
-        for t in range(PACK):
+        A("S", 0, 1, 0, 256)
+        A("V", 0, 1, 256, 512)
+        for t in range(2):
             M1(0, 0, t, (0,))
-        A("S", 0, 1, 0, 320)
-        A("V", 0, 1, 320, 512)
-        CW(0, 1, 1)
+        CW(0, 0, 1)
         B(0, 1)
         for t in range(PACK):
-            M1(0, 0, t, (1,))
+            M1(0, 0, t, (1,) if t < 2 else (0, 1))
+        CW(0, 1, 1)
+        A("S", 1, 0)
         cw = [(b, h, g) for b in range(1, L) for h in range(G) for g in range(G)]
 
         def finish(b, a):
@@ -279,15 +336,17 @@ def tile_layerwise_subspace_newton_matrix_k7_kernel(
             store_y(b, a)
 
         def prefetch(s):
-            b, h = divmod(s, G)
-            A("G", b + 1, h, 0, AG[s])
+            if s < 5:
+                A("G", *divmod(s + 3, G), 0, AG[s])
+            else:
+                K(0, 2, "G", 0, 1)
             for i in range(NG[s]):
                 CW(*cw.pop(0), "G")
+            if s < 5:
+                A("S", *divmod(s + 3, G), AG[s], R)
 
         def fills(s):
             b, h = divmod(s, G)
-            if AS[s] < R:
-                A("V", b + 1, h, AS[s], R)
             if s == 1:
                 CW(*cw.pop(0))
                 B(b + 1, h)
@@ -298,43 +357,37 @@ def tile_layerwise_subspace_newton_matrix_k7_kernel(
             if h == 0 and b > 0:
                 M2(b - 1, 0)
                 M2(b - 1, 1)
-            if b > 1:
-                I(b - 2, 256 * h, 256 * h + 256)
-                store_codes(b - 2, 256 * h, 256 * h + 256)
+            if s == 5:
+                I(0, 0, 256)
+                store_codes(0, 0, 256)
             for i in range(NCW[s]):
                 CW(*cw.pop(0))
             if s != 1:
                 B(b + 1, h)
 
-        CW(*cw.pop(0))
         for b in range(L - 1):
             s = 2 * b
             prefetch(s)
             if b > 1:
-                K(b - 2, 0)
-                K(b - 2, 1)
-                T(b - 2, 0)
-                T(b - 2, 1)
-            A("S", b + 1, 0, AG[s], AS[s])
-            if b > 1:
                 finish(b - 2, 2)
                 finish(b - 2, 3)
-                H(b - 2, 0, 2)
-                K(b - 2, 2)
-                K(b - 2, 3)
+                K(b - 2, 0)
+                K(b - 2, 1)
             for t in range(PACK):
                 Dd(b, 0, t)
                 M1(b, 1, t)
             J("S", b, 0, 0)
             J("S", b, 0, 1)
+            if b > 1:
+                T(b - 2, 0)
+                T(b - 2, 1)
             fills(s)
             s += 1
             prefetch(s)
             if b > 1:
-                T(b - 2, 2)
-                T(b - 2, 3)
-                H(b - 2, 2, 4)
-            A("S", b + 1, 1, AG[s], AS[s])
+                H(b - 2, 0, 2)
+                K(b - 2, 2, "S", 1, 2)
+                K(b - 2, 3)
             for t in range(PACK):
                 Dd(b, 1, t)
                 M1(b + 1, 0, t, (0,))
@@ -344,6 +397,10 @@ def tile_layerwise_subspace_newton_matrix_k7_kernel(
                 for a in (0, 1):
                     finish(b - 1, a)
                     M2(b - 1, a + 2)
+            if b > 1:
+                T(b - 2, 2)
+                T(b - 2, 3)
+                H(b - 2, 2, 4)
             fills(s)
             if s != 1:
                 for t in range(PACK):
@@ -360,6 +417,8 @@ def tile_layerwise_subspace_newton_matrix_k7_kernel(
         for t in range(PACK):
             if t == 3:
                 E(b - 1, 1)
+                I(0, 256, 512)
+                store_codes(0, 256, 512)
                 M2(b - 1, 0)
                 M2(b - 1, 1)
             Dd(b, 0, t)
@@ -388,41 +447,44 @@ def tile_layerwise_subspace_newton_matrix_k7_kernel(
         H(b - 2, 2, 4)
         T(b - 1, 0)
         T(b - 1, 1)
+        E(b, 0)
+        for a in range(RT):
+            M2(b, a, (0,))
         finish(b - 1, 2)
         K(b - 1, 2)
-        E(b, 0)
         E(b, 1, 0, 256)
-        M2(b, 0)
-        M2(b, 1)
+        M2(b, 0, (1,))
+        M2(b, 1, (1,))
         J("V", b, 1, 1, 128, 256)
         finish(b - 1, 3)
         E(b, 1, 256, 512)
-        M2(b, 2)
-        M2(b, 3)
+        M2(b, 2, (1,))
+        M2(b, 3, (1,))
         K(b - 1, 3)
         H(b - 1, 0, 2)
         T(b - 1, 2)
         T(b - 1, 3)
         I(b - 2)
         store_codes(b - 2)
-        store_scales(0, R * (b - 1), nc.sync)
+        store_scales(0, R * (b - 1), [nc.sync])
         finish(b, 0)
         K(b, 0)
         H(b - 1, 2, 4)
-        for a in range(1, RT):
+        for a in (1, 2):
             finish(b, a)
-            if a < 3:
-                K(b, a)
+            K(b, a)
+        FK(b, 3)
+        finish(b, 3)
+        for a in (0, 1, 3, 2):
+            T(b, a)
         I(b - 1)
         store_codes(b - 1)
-        K(b, 3, "V")
-        for a in range(RT):
-            T(b, a)
-        for a in range(RT):
-            H(b, a, a + 1, "V" if a == 3 else "S")
-            if a == 1:
-                I(b, 0, 256)
-                store_codes(b, 0, 256)
+        H(b, 0, 1)
+        H(b, 1, 2)
+        H(b, 3, 4, "V")
+        H(b, 2, 3)
+        I(b, 0, 256)
+        store_codes(b, 0, 256)
         I(b, 256, 512)
         store_codes(b, 256, 512)
-        store_scales(R * (b - 1), R * L, nc.scalar)
+        store_scales(R * (b - 1), R * L, [nc.scalar, nc.sync])

from contextlib import ExitStack

import concourse.mybir as mybir
from concourse.masks import make_identity

L, D, R = 4, 1024, 512
FLOPS = L * (2 * R * D * D + 2 * R * D * R)

F32 = mybir.dt.float32
BF16 = mybir.dt.bfloat16
I32 = mybir.dt.int32
U32 = mybir.dt.uint32
U8 = mybir.dt.uint8
FP8X4 = mybir.dt.float8_e4m3fn_x4
FP4X4 = mybir.dt.float4_e2m1fn_x4
MULT = mybir.AluOpType.mult
ADD = mybir.AluOpType.add

P = 128
PACK = 4
G = D // (P * PACK)
RT = R // P
NSIL = 2
NHC = 4
AG = [128, 128, 32, 32, 32]
NG = [1, 1, 1, 2, 2, 2]
NCW = [1, 0, 1, 0, 0, 0]
ALIAS = {(0, 2): 0}
WN = 128
DIRECT = set()


def tile_layerwise_subspace_newton_matrix_k7_kernel(
    tc, dirs, h_words, h_scales, ridge, prev, carry, out_0, out_1, out_2
):
    nc = tc.nc
    with ExitStack() as ctx:
        sb = ctx.enter_context(tc.tile_pool(name="sb", bufs=1))
        ps = ctx.enter_context(tc.psum_pool(name="ps", bufs=1))

        def tiles(name, count, shape, dtype):
            return [sb.tile(shape, dtype, name="%s%d" % (name, i), align_bytes=64) for i in range(count)]

        s_raw = tiles("s_raw", L * G, [P, PACK, R], BF16)
        s_il = tiles("s_il", NSIL, [P, R, PACK], BF16)
        s_codes = tiles("s_codes", L * G, [P, R], U32)
        s_scales = tiles("s_scales", L * G, [P, R], U8)
        h_raw = tiles("h_raw", L * G, [P, 2 * D], U8)
        h_cols = tiles("h_cols", NHC * G, [P, G, PACK, 2 * P], U8)
        hs_raw = tiles("hs_raw", 1, [P, D], U8)[0]
        hs_cols = tiles("hs_cols", L * G, [P, D], U8)
        m_raw = tiles("m_raw", L, [P, RT, R], BF16)
        d_rows = tiles("d_rows", 1, [P, 512], BF16)[0]
        d_col = tiles("d_col", 1, [P, L * G, PACK], BF16)[0]
        mu = tiles("mu", 1, [P, L], BF16)[0]
        ident = tiles("ident", 1, [P, P], F32)[0]
        u_rows = tiles("u_rows", 2 * G, [P, 2, PACK, R // 2], BF16)
        u_il = tiles("u_il", 2 * G, [P, R, PACK], BF16)
        u_codes = tiles("u_codes", 2 * G, [P, R], U32)
        u_scales = tiles("u_scales", 2 * G, [P, R], U8)
        y = tiles("y", 2 * RT, [P, R], F32)
        y_bf = tiles("y_bf", 2 * RT, [P, R], BF16)
        y_il = tiles("y_il", 2, [P, R, PACK], BF16)
        y_codes = tiles("y_codes", L, [P, R], U32)
        y_scales = tiles("y_scales", 1, [P, L * R], U8)[0]
        u_bank = [ps.tile([P, R], F32, name="u_bank%d" % i) for i in range(PACK)]
        a_bank = [ps.tile([P, R], F32, name="a_bank%d" % i) for i in range(2)]
        t_bank = [ps.tile([P, R], F32, name="t_bank%d" % i) for i in range(2)]

        def abank(b, a):
            return u_bank[a] if b == L - 1 else a_bank[a % 2]

        def tbank(b, a):
            return [t_bank[0], a_bank[0], t_bank[1], a_bank[1]][a] if b == L - 1 else t_bank[a % 2 if DIRECT else a // 2]

        def sbuf(k):
            return k % 2 if k < 2 else (k + 1) % 2

        def load_s(b, g):
            rows = dirs[b, 512 * g : 512 * (g + 1), :]
            nc.sync.dma_start(out=s_raw[G * b + g][:], in_=rows.rearrange("(p t) r -> p t r", t=PACK))

        def load_h(b, g):
            nc.sync.dma_start(out=h_raw[G * b + g][:].bitcast(I32), in_=h_words[G * b + g].bitcast(I32))

        def load_hs():
            for q in range(4):
                nc.sync.dma_start(
                    out=hs_raw[32 * q : 32 * (q + 1), :].bitcast(I32),
                    in_=h_scales[:, 4 * q : 4 * q + 4, :].bitcast(I32),
                )

        def shift_hs(k, eng):
            eng.dma_start(out=hs_cols[k][0:100, :].bitcast(I32), in_=hs_cols[0][4 * k : 4 * k + 100, :].bitcast(I32))

        def load_d():
            nc.sync.dma_start(out=d_rows[0 : L * G, :], in_=ridge.rearrange("b (g j) -> (b g) j", g=G))

        def turn_d():
            for u in range(2):
                nc.tensor.transpose(a_bank[0][:, P * u : P * (u + 1)], d_rows[:].bitcast(F32)[:, u:256:2], ident[:])

        def copy_d():
            nc.scalar.copy(
                out=d_col[:].rearrange("p k t -> p (k t)").bitcast(F32).rearrange("p (k u) -> p k u", u=2),
                in_=a_bank[0][:, 0:256].rearrange("p (u k) -> p k u", u=2)[:, 0 : L * G, :],
            )

        def load_m(b):
            nc.sync.dma_start(out=m_raw[b][:], in_=prev[b].rearrange("(a p) s -> p a s", p=P))

        def interleave(eng, dst, src, c0, c1):
            out = dst[:, c0:c1, :].rearrange("p (c i) t -> p c t i", i=4)
            in_ = src[:, :, c0:c1].rearrange("p t (c i) -> p c t i", i=4)
            if eng == "V":
                nc.vector.tensor_copy(out=out, in_=in_)
            elif eng == "S":
                nc.scalar.copy(out=out, in_=in_)
            else:
                nc.gpsimd.tensor_scalar(out=out, in0=in_, scalar1=1.0, scalar2=0.0, op0=MULT, op1=ADD)

        def A(eng, b, g, c0=0, c1=R):
            interleave(eng, s_il[(G * b + g) % 2], s_raw[G * b + g], c0, c1)

        def B(b, g):
            k = G * b + g
            nc.vector.quantize_mx(
                out=s_codes[k][:].bitcast(FP8X4),
                scales=s_scales[k][:],
                in_=s_il[k % 2][:].rearrange("p r t -> p (r t)"),
            )

        def CW(b, h, g, eng="V"):
            src = h_raw[G * b + g][:, D * h : D * (h + 1)].rearrange("p (m t e) -> p t m e", t=PACK, e=2)
            dst = h_cols[G * (b % NHC) + h][:, g, :, :].rearrange("p t (m e) -> p t m e", e=2)
            (nc.vector if eng == "V" else nc.gpsimd).tensor_copy(out=dst, in_=src)

        def CS():
            src = hs_raw[:].rearrange("p (h m t) -> p h t m", h=G, t=PACK)
            dst = hs_cols[0][:].rearrange("p (h t m) -> p h t m", h=G, t=PACK)
            nc.vector.tensor_copy(out=dst, in_=src)

        def M1(b, h, t, gs=(0, 1)):
            for g in gs:
                nc.tensor.matmul_mx(
                    out=u_bank[t][:],
                    lhsT=h_cols[G * (b % NHC) + h][:, g, t, :].bitcast(FP4X4),
                    lhsT_scale=hs_cols[G * b + g][:, P * (PACK * h + t) : P * (PACK * h + t + 1)],
                    rhs=s_codes[G * b + g][:].bitcast(FP8X4),
                    rhs_scale=s_scales[G * b + g][:],
                    start=(g == 0),
                    stop=(g == G - 1),
                )

        def Dd(b, h, t, f0=0, f1=2):
            cols = slice(256 * f0, 256 * f1)
            nc.vector.scalar_tensor_tensor(
                out=u_rows[G * (b % 2) + h][:, f0:f1, t, :],
                in0=s_raw[G * b + h][:, t, cols].rearrange("p (f r) -> p f r", r=256),
                scalar=d_col[:, G * b + h, t : t + 1],
                in1=u_bank[t][:, cols].rearrange("p (f r) -> p f r", r=256),
                op0=MULT,
                op1=ADD,
            )

        def J(eng, b, h, f, c0=0, c1=256):
            k = G * (b % 2) + h
            interleave(eng, u_il[k][:, 256 * f : 256 * (f + 1), :], u_rows[k][:, f, :, :], c0, c1)

        def E(b, h, c0=0, c1=R):
            k = G * (b % 2) + h
            nc.vector.quantize_mx(
                out=u_codes[k][:, c0:c1].bitcast(FP8X4),
                scales=u_scales[k][:, c0:c1],
                in_=u_il[k][:, c0:c1, :].rearrange("p r t -> p (r t)"),
            )

        def M2(b, a, hs=(0, 1)):
            cols = slice(P * a, P * (a + 1))
            for h in hs:
                k = G * (b % 2) + h
                nc.tensor.matmul_mx(
                    out=abank(b, a)[:],
                    lhsT=u_codes[k][:, cols].bitcast(FP8X4),
                    lhsT_scale=u_scales[k][:, cols],
                    rhs=s_codes[G * b + h][:].bitcast(FP8X4),
                    rhs_scale=s_scales[G * b + h][:],
                    start=(h == 0),
                    stop=(h == G - 1),
                )

        def F(b, a):
            nc.vector.scalar_tensor_tensor(
                out=y[RT * (b % 2) + a][:],
                in0=m_raw[b][:, a, :],
                scalar=mu[:, b : b + 1],
                in1=abank(b, a)[:],
                op0=MULT,
                op1=ADD,
            )

        def store_y(b, a):
            nc.sync.dma_start(out=out_0[b, P * a : P * (a + 1), :], in_=y[RT * (b % 2) + a][:])

        def ybf(b, a):
            if (b, a) in ALIAS:
                return s_il[ALIAS[(b, a)]][:, 0:P, :].rearrange("p r t -> p (r t)")
            return y_bf[RT * (b % 2) + a][:]

        def K(b, a, eng="S", u0=0, u1=2):
            if (b, a) in DIRECT:
                return
            out = ybf(b, a).rearrange("r (u p e) -> r u p e", u=2, e=2)[:, u0:u1]
            in_ = y[RT * (b % 2) + a][:].rearrange("r (p u e) -> r u p e", u=2, e=2)[:, u0:u1]
            if eng == "V":
                nc.vector.tensor_copy(out=out, in_=in_)
            elif eng == "S":
                nc.scalar.copy(out=out, in_=in_)
            else:
                nc.gpsimd.tensor_scalar(out=out, in0=in_, scalar1=1.0, scalar2=0.0, op0=MULT, op1=ADD)

        def FK(b, a):
            for u in range(2):
                nc.vector.scalar_tensor_tensor(
                    out=ybf(b, a)[:, 256 * u : 256 * (u + 1)].rearrange("r (p e) -> r p e", e=2),
                    in0=m_raw[b][:, a, :].rearrange("r (p u e) -> r u p e", u=2, e=2)[:, u],
                    scalar=mu[:, b : b + 1],
                    in1=abank(b, a)[:].rearrange("r (p u e) -> r u p e", u=2, e=2)[:, u],
                    op0=MULT,
                    op1=ADD,
                )

        def T(b, a):
            if (b, a) in DIRECT:
                for t in range(PACK):
                    nc.tensor.transpose(tbank(b, a)[:, P * t : P * (t + 1)], y[RT * (b % 2) + a][:, t:R:PACK], ident[:])
                return
            for u in range(2):
                c = P * (2 * (a % 2) + u)
                nc.tensor.transpose(
                    tbank(b, a)[:, c : c + P], ybf(b, a).bitcast(F32)[:, P * u : P * (u + 1)], ident[:]
                )

        def H(b, a0, a1, eng="S"):
            if DIRECT and a1 - a0 == 2:
                H(b, a0, a0 + 1, eng)
                H(b, a0 + 1, a1, eng)
                return
            if (b, a0) in DIRECT:
                nc.scalar.copy(
                    out=y_il[b % 2][:, P * a0 : P * a1, :], in_=tbank(b, a0)[:].rearrange("p (t r) -> p r t", t=PACK)
                )
                return
            copy = nc.scalar.copy if eng == "S" else nc.vector.tensor_copy
            words = y_il[b % 2][:, P * a0 : P * a1, :].rearrange("p r t -> p (r t)").bitcast(F32)
            src = tbank(b, a0)[:, 2 * P * (a0 % 2) : 2 * P * (a0 % 2 + a1 - a0)]
            copy(
                out=words.rearrange("p (a r u) -> p a r u", r=P, u=2),
                in_=src.rearrange("p (a u r) -> p a r u", r=P, u=2),
            )

        def I(b, c0=0, c1=R):
            nc.vector.quantize_mx(
                out=y_codes[b][:, c0:c1].bitcast(FP8X4),
                scales=y_scales[:, R * b + c0 : R * b + c1],
                in_=y_il[b % 2][:, c0:c1, :].rearrange("p r t -> p (r t)"),
            )

        def store_codes(b, c0=0, c1=R):
            dst = out_1[0, :, R * b + c0 : R * b + c1, :].rearrange("p m t -> p (m t)").bitcast(I32)
            nc.sync.dma_start(out=dst, in_=y_codes[b][:, c0:c1].bitcast(I32))

        def store_scales(c0, c1, engs):
            for q in range(4):
                engs[q % len(engs)].dma_start(
                    out=out_2[0, 4 * q : 4 * q + 4, c0:c1].bitcast(I32),
                    in_=y_scales[32 * q : 32 * q + 4, c0:c1].bitcast(I32),
                )

        ctx.enter_context(tc.manual_schedule())

        make_identity(nc, ident[:])
        nc.vector.memset(d_rows[:].bitcast(I32), 0)
        for k in range(1, L * G):
            nc.vector.memset(hs_cols[k][:].bitcast(I32), 0)
        load_hs()
        load_d()
        turn_d()
        copy_d()
        load_h(0, 0)
        load_s(0, 0)
        load_s(0, 1)
        load_h(0, 1)
        CS()
        shift_hs(1, nc.sync)
        load_s(1, 0)
        load_h(1, 0)
        load_s(1, 1)
        load_h(1, 1)
        for k in range(2, 4):
            shift_hs(k, nc.sync)
        load_s(2, 0)
        load_m(0)
        nc.sync.dma_start(out=mu[:], in_=carry.partition_broadcast(P))
        load_h(2, 0)
        load_h(2, 1)
        load_s(2, 1)
        for k in range(4, L * G):
            shift_hs(k, nc.sync)
        load_s(3, 0)
        load_h(3, 0)
        load_h(3, 1)
        load_s(3, 1)
        for b in range(1, L):
            load_m(b)

        CW(0, 0, 0)
        CW(0, 1, 0)
        A("S", 0, 0, 0, 192)
        A("V", 0, 0, 192, 512)
        B(0, 0)
        A("S", 0, 1, 0, 256)
        A("V", 0, 1, 256, 512)
        for t in range(2):
            M1(0, 0, t, (0,))
        CW(0, 0, 1)
        B(0, 1)
        for t in range(PACK):
            M1(0, 0, t, (1,) if t < 2 else (0, 1))
        CW(0, 1, 1)
        A("S", 1, 0)
        cw = [(b, h, g) for b in range(1, L) for h in range(G) for g in range(G)]

        def finish(b, a):
            F(b, a)
            store_y(b, a)

        def prefetch(s):
            if s < 5:
                A("G", *divmod(s + 3, G), 0, AG[s])
            else:
                K(0, 2, "G", 0, 1)
            for i in range(NG[s]):
                CW(*cw.pop(0), "G")
            if s < 5:
                A("S", *divmod(s + 3, G), AG[s], R)

        def fills(s):
            b, h = divmod(s, G)
            if s == 1:
                CW(*cw.pop(0))
                B(b + 1, h)
                for t in range(PACK):
                    M1(b + 1, 0, t, (1,))
            if s > 0:
                E(*divmod(s - 1, G))
            if h == 0 and b > 0:
                M2(b - 1, 0)
                M2(b - 1, 1)
            if s == 5:
                I(0, 0, 256)
                store_codes(0, 0, 256)
            for i in range(NCW[s]):
                CW(*cw.pop(0))
            if s != 1:
                B(b + 1, h)

        for b in range(L - 1):
            s = 2 * b
            prefetch(s)
            if b > 1:
                finish(b - 2, 2)
                finish(b - 2, 3)
                K(b - 2, 0)
                K(b - 2, 1)
            for t in range(PACK):
                Dd(b, 0, t)
                M1(b, 1, t)
            J("S", b, 0, 0)
            J("S", b, 0, 1)
            if b > 1:
                T(b - 2, 0)
                T(b - 2, 1)
            fills(s)
            s += 1
            prefetch(s)
            if b > 1:
                H(b - 2, 0, 2)
                K(b - 2, 2, "S", 1, 2)
                K(b - 2, 3)
            for t in range(PACK):
                Dd(b, 1, t)
                M1(b + 1, 0, t, (0,))
            J("S", b, 1, 0)
            J("S", b, 1, 1)
            if b > 0:
                for a in (0, 1):
                    finish(b - 1, a)
                    M2(b - 1, a + 2)
            if b > 1:
                T(b - 2, 2)
                T(b - 2, 3)
                H(b - 2, 2, 4)
            fills(s)
            if s != 1:
                for t in range(PACK):
                    M1(b + 1, 0, t, (1,))
        assert not cw

        b = L - 1
        K(b - 2, 0)
        K(b - 2, 1)
        finish(b - 2, 2)
        finish(b - 2, 3)
        K(b - 2, 2, "G")
        K(b - 2, 3, "G")
        for t in range(PACK):
            if t == 3:
                E(b - 1, 1)
                I(0, 256, 512)
                store_codes(0, 256, 512)
                M2(b - 1, 0)
                M2(b - 1, 1)
            Dd(b, 0, t)
            M1(b, 1, t)
            if t == 1:
                T(b - 2, 0)
                T(b - 2, 1)
                H(b - 2, 0, 2)
        J("S", b, 0, 0)
        J("S", b, 0, 1)
        T(b - 2, 2)
        T(b - 2, 3)
        Dd(b, 1, 0, 0, 1)
        Dd(b, 1, 1, 0, 1)
        for a in (0, 1):
            finish(b - 1, a)
            K(b - 1, a, "G")
            M2(b - 1, a + 2)
        Dd(b, 1, 2, 0, 1)
        Dd(b, 1, 3, 0, 1)
        J("S", b, 1, 0, 0, 128)
        J("S", b, 1, 0, 128, 256)
        for t in range(PACK):
            Dd(b, 1, t, 1, 2)
        J("S", b, 1, 1, 0, 128)
        H(b - 2, 2, 4)
        T(b - 1, 0)
        T(b - 1, 1)
        E(b, 0)
        for a in range(RT):
            M2(b, a, (0,))
        finish(b - 1, 2)
        K(b - 1, 2)
        E(b, 1, 0, 256)
        M2(b, 0, (1,))
        M2(b, 1, (1,))
        J("V", b, 1, 1, 128, 256)
        finish(b - 1, 3)
        E(b, 1, 256, 512)
        M2(b, 2, (1,))
        M2(b, 3, (1,))
        K(b - 1, 3)
        H(b - 1, 0, 2)
        T(b - 1, 2)
        T(b - 1, 3)
        I(b - 2)
        store_codes(b - 2)
        store_scales(0, R * (b - 1), [nc.sync])
        finish(b, 0)
        K(b, 0)
        H(b - 1, 2, 4)
        for a in (1, 2):
            finish(b, a)
            K(b, a)
        FK(b, 3)
        finish(b, 3)
        for a in (0, 1, 3, 2):
            T(b, a)
        I(b - 1)
        store_codes(b - 1)
        H(b, 0, 1)
        H(b, 1, 2)
        H(b, 3, 4, "V")
        H(b, 2, 3)
        I(b, 0, 256)
        store_codes(b, 0, 256)
        I(b, 256, 512)
        store_codes(b, 256, 512)
        store_scales(R * (b - 1), R * L, [nc.scalar, nc.sync])
